import numpy as np
import ml_dtypes


def mxq(x, axis, fmt="e4m3"):
    dtype, down = {"e4m3": (ml_dtypes.float8_e4m3fn, 7), "e5m2": (ml_dtypes.float8_e5m2, 14)}[fmt]
    v = np.moveaxis(np.asarray(x, np.float32).astype(ml_dtypes.bfloat16).astype(np.float64), axis, -1)
    blocks = v.reshape(v.shape[:-1] + (-1, 32))
    amax = np.abs(blocks).max(-1, keepdims=True)
    byte = np.maximum(np.where(amax > 0, np.frexp(amax)[1] - 1 + 127, 0) - down, 1)
    scale = np.exp2(byte - 127.0)
    codes = (blocks / scale).astype(np.float32).astype(dtype).astype(np.float64)
    return np.moveaxis((codes * scale).reshape(v.shape), -1, axis)


WIDE = False


def mx_kscale(k):
    if not WIDE:
        return np.ones(k)
    levels = np.array([10, -10, 5, -5, 0])
    if k % 512:
        return np.exp2(np.random.permutation(np.resize(levels, k // 32))).repeat(32)
    a = np.empty((k // 512, 16))
    for p in range(k // 512):
        a[p, :8] = np.random.permutation(np.resize(levels, 8))
        for g in range(8):
            far = levels[np.abs(levels - a[p, g]) >= 10]
            a[p, g + 8] = far[np.random.randint(len(far))]
    return np.exp2(a.ravel()).repeat(32)


def f64(x):
    return np.asarray(x).astype(np.float64)


def striped(idx):
    return np.tile(idx.reshape(-1, 16).T, (8, 1)).astype(np.uint16)


def unstriped(offs):
    return offs[:16].T.reshape(-1).astype(np.int64)


def gelu(v):
    return 0.5 * v * (1.0 + np.tanh(np.sqrt(2.0 / np.pi) * (v + 0.044715 * v**3)))


K, T, D, S, V, H, N = 1024, 2048, 3, 768, 384, 512, 128


def setup_inputs():
    n = np.random.standard_normal
    s = mx_kscale(K)[:, None]
    u = mx_kscale(H)
    return {
        "xT": (n((K, T)) * s).astype(np.float32),
        "w1": (n((K, H)) / np.sqrt(K) / s * u).astype(np.float32),
        "w2": (n((H, N)) / np.sqrt(H) / u[:, None]).astype(np.float32),
        "gate": np.tile(np.random.uniform(0.2, 1.0, (D, 1, V)) / np.sqrt(D), (1, N, 1)).astype(np.float32),
        "offs": striped(np.random.permutation(T)[:S]),
        "pos1": striped(np.random.permutation(S)[:V]),
        "pos2": striped(np.random.permutation(S)[:V]),
        "pos3": striped(np.random.permutation(S)[:V]),
    }


def reference(xT, w1, w2, gate, offs, pos1, pos2, pos3):
    idx = unstriped(offs)
    xq = mxq(f64(xT)[:, idx], 0, "e4m3")
    h = gelu(mxq(f64(w1), 0, "e4m3").T @ xq)
    y = mxq(f64(w2), 0, "e4m3").T @ mxq(h, 0, "e4m3")
    return sum(f64(gate[d]) * y[:, unstriped(p)] for d, p in enumerate((pos1, pos2, pos3)))

@@ -1,0 +1,229 @@
+from contextlib import ExitStack
+
+import concourse.mybir as mybir
+
+K, T, D, S, V, H, N = 1024, 2048, 3, 768, 384, 512, 128
+FLOPS = 2 * K * H * S + 2 * H * N * S
+
+F32 = mybir.dt.float32
+BF16 = mybir.dt.bfloat16
+U32 = mybir.dt.uint32
+U16 = mybir.dt.uint16
+U8 = mybir.dt.uint8
+FP8X4 = mybir.dt.float8_e4m3fn_x4
+MULT = mybir.AluOpType.mult
+GELU = mybir.ActivationFunctionType.Gelu_apprx_tanh
+
+P = 128
+PACK = 4
+K_PASS = P * PACK
+PASSES = K // K_PASS
+SLICE = 128
+SLICES = S // SLICE
+
+
+def tile_picked_sub_mlp_gelu_sub_e_kernel(
+    tc, xT, w1, w2, gate, offs, pos1, pos2, pos3, out
+):
+    nc = tc.nc
+    with ExitStack() as ctx:
+        keep = ctx.enter_context(tc.tile_pool(name="keep", bufs=1))
+        ring = ctx.enter_context(tc.tile_pool(name="ring", bufs=3))
+        banks = ctx.enter_context(tc.psum_pool(name="banks", bufs=1))
+        ybanks = ctx.enter_context(tc.psum_pool(name="ybanks", bufs=2))
+
+        dummy = keep.tile([P, 1], F32, name="dummy")
+        nc.vector.memset(dummy[:], 0.0)
+        dummy_out = keep.tile([P, 1], F32, name="dummy_out")
+        nc.scalar.activation(dummy_out[:], dummy[:], GELU)
+
+        planes = []
+        offsets = keep.tile([P, S // 16], U16, name="offsets")
+        for s in range(PASSES):
+            rows = xT[s * K_PASS : (s + 1) * K_PASS, :].rearrange("(p t) c -> p t c", t=PACK)
+            for t in range(PACK):
+                plane = keep.tile([P, T], F32, name=f"plane{s}{t}")
+                nc.sync.dma_start(plane[:], rows[:, t, :])
+                planes.append(plane)
+                if s == 0 and t == 0:
+                    nc.sync.dma_start(offsets[:], offs)
+        w1_raw = []
+        for s in range(PASSES):
+            rows = w1[s * K_PASS : (s + 1) * K_PASS, :].rearrange("(p j) c -> p j c", j=PACK)
+            for u in range(2):
+                raw = keep.tile([P, 2, H], F32, name=f"w1raw{s}{u}")
+                nc.sync.dma_start(raw[:], rows[:, 2 * u : 2 * u + 2, :])
+                w1_raw.append(raw)
+        w2_raw = keep.tile([P, PACK, N], F32, name="w2_raw")
+        nc.sync.dma_start(w2_raw[:], w2.rearrange("(p j) n -> p j n", j=PACK))
+        places = []
+        for d, pos in enumerate((pos1, pos2, pos3)):
+            place = keep.tile([P, V // 16], U16, name=f"place{d}")
+            nc.sync.dma_start(place[:], pos)
+            places.append(place)
+        gates = keep.tile([P, D, V], F32, name="gates")
+        nc.sync.dma_start(gates[:], gate.rearrange("d m v -> m d v"))
+
+        x_codes = []
+        x_scales = []
+        for s in range(PASSES):
+            x_codes.append(keep.tile([P, S], U32, align_bytes=64, name=f"x_codes{s}"))
+            x_scales.append(keep.tile([P, S], U8, align_bytes=64, name=f"x_scales{s}"))
+
+        def quantise_x(s, grouped):
+            for a, b in ((0, 512), (512, 768)):
+                nc.vector.quantize_mx(
+                    out=x_codes[s][:, a:b].bitcast(FP8X4),
+                    scales=x_scales[s][:, a:b],
+                    in_=grouped[:, a:b, :].rearrange("p n t -> p (n t)"),
+                )
+
+        xg0 = keep.tile([P, S, PACK], BF16, align_bytes=64, name="xg0")
+        xg1 = keep.tile([P, S, PACK], BF16, align_bytes=64, name="xg1")
+        picked0 = keep.tile([P, PACK, S], F32, name="picked0")
+        picked1 = keep.tile([P, 2, S], F32, name="picked1")
+        for t in range(PACK):
+            nc.vector.tensor_copy(picked0[:, t, :], planes[t][:].indirect(offsets[:]))
+        nc.scalar.copy(
+            xg0[:].rearrange("p (c i) t -> p c t i", i=4),
+            picked0[:].rearrange("p t (c i) -> p c t i", i=4),
+        )
+        for t in range(2):
+            nc.vector.tensor_copy(picked1[:, t, :], planes[4 + t][:].indirect(offsets[:]))
+        nc.scalar.copy(xg1[:, :, 0:2], picked1[:].rearrange("p t n -> p n t"))
+        quantise_x(0, xg0)
+        for t in range(2, PACK):
+            nc.vector.tensor_copy(xg1[:, :, t], planes[4 + t][:].indirect(offsets[:]))
+        quantise_x(1, xg1)
+
+        w1_codes = []
+        w1_scales = []
+        w1_grouped = []
+        for s in range(PASSES):
+            w1_codes.append(keep.tile([P, H], U32, align_bytes=64, name=f"w1_codes{s}"))
+            w1_scales.append(keep.tile([P, H], U8, align_bytes=64, name=f"w1_scales{s}"))
+            w1_grouped.append(keep.tile([P, PACK, P, PACK], BF16, align_bytes=64, name=f"w1_grouped{s}"))
+
+        def group_w1(copy, s, u, a, b):
+            copy(
+                w1_grouped[s][:, :, a:b, 2 * u : 2 * u + 2].rearrange("p t m j -> p m t j"),
+                w1_raw[2 * s + u][:, :, PACK * a : PACK * b].rearrange("p j (m t) -> p m t j", t=PACK),
+            )
+
+        def quantise_w1(s):
+            for a, b in ((0, 2), (2, 4)):
+                nc.vector.quantize_mx(
+                    out=w1_codes[s][:, P * a : P * b].bitcast(FP8X4),
+                    scales=w1_scales[s][:, P * a : P * b],
+                    in_=w1_grouped[s][:, a:b].rearrange("p t m j -> p (t m j)"),
+                )
+
+        group_w1(nc.scalar.copy, 0, 0, 0, P)
+        group_w1(nc.scalar.copy, 0, 1, 0, 64)
+        group_w1(nc.vector.tensor_copy, 0, 1, 64, P)
+        quantise_w1(0)
+        group_w1(nc.scalar.copy, 1, 0, 0, P)
+        group_w1(nc.scalar.copy, 1, 1, 0, 40)
+        group_w1(nc.vector.tensor_copy, 1, 1, 40, P)
+        quantise_w1(1)
+
+        w2_grouped = keep.tile([P, N, PACK], BF16, align_bytes=64, name="w2_grouped")
+        w2_codes = keep.tile([P, N], U32, align_bytes=64, name="w2_codes")
+        w2_scales = keep.tile([P, N], U8, align_bytes=64, name="w2_scales")
+        nc.vector.tensor_copy(w2_grouped[:], w2_raw[:].rearrange("p j n -> p n j"))
+        nc.vector.quantize_mx(
+            out=w2_codes[:].bitcast(FP8X4),
+            scales=w2_scales[:],
+            in_=w2_grouped[:].rearrange("p n j -> p (n j)"),
+        )
+
+        acc = []
+        for i in range(SLICES):
+            acc.append(banks.tile([P, PACK, SLICE], F32, name=f"acc{i}"))
+
+        def layer1(i, t, s):
+            cols = slice(i * SLICE, (i + 1) * SLICE)
+            nc.tensor.matmul_mx(
+                out=acc[i][:, t, :],
+                lhsT=w1_codes[s][:, t * P : (t + 1) * P].bitcast(FP8X4),
+                lhsT_scale=w1_scales[s][:, t * P : (t + 1) * P],
+                rhs=x_codes[s][:, cols].bitcast(FP8X4),
+                rhs_scale=x_scales[s][:, cols],
+                start=(s == 0),
+                stop=(s == PASSES - 1),
+            )
+
+        y = keep.tile([P, S], F32, name="y")
+        hidden = []
+
+        def layer2(i):
+            h_codes, h_scales = hidden[i]
+            y_bank = ybanks.tile([P, SLICE], F32, name="y_bank")
+            nc.tensor.matmul_mx(
+                out=y_bank[:],
+                lhsT=w2_codes[:].bitcast(FP8X4),
+                lhsT_scale=w2_scales[:],
+                rhs=h_codes[:].bitcast(FP8X4),
+                rhs_scale=h_scales[:],
+                start=True,
+                stop=True,
+            )
+            nc.vector.tensor_copy(y[:, i * SLICE : (i + 1) * SLICE], y_bank[:])
+
+        for r in range(3):
+            warm = ybanks.tile([P, 512], F32, name="y_bank")
+            nc.tensor.matmul_mx(
+                out=warm[:],
+                lhsT=x_codes[0][:, 0:P].bitcast(FP8X4),
+                lhsT_scale=x_scales[0][:, 0:P],
+                rhs=x_codes[1][:, 0:512].bitcast(FP8X4),
+                rhs_scale=x_scales[1][:, 0:512],
+                start=True,
+                stop=True,
+            )
+        for i in range(SLICES):
+            layer1(i, 0, 0)
+        for i in range(SLICES):
+            layer1(i, 0, 1)
+            for t in range(1, PACK):
+                for s in range(PASSES):
+                    layer1(i, t, s)
+            h = ring.tile([P, SLICE, PACK], BF16, align_bytes=64, name="h")
+            nc.scalar.activation(h[:], acc[i][:].rearrange("p t n -> p n t"), GELU)
+            h_codes = ring.tile([P, SLICE], U32, align_bytes=64, name="h_codes")
+            h_scales = ring.tile([P, SLICE], U8, align_bytes=64, name="h_scales")
+            nc.vector.quantize_mx(
+                out=h_codes[:].bitcast(FP8X4),
+                scales=h_scales[:],
+                in_=h[:].rearrange("p n t -> p (n t)"),
+            )
+            hidden.append((h_codes, h_scales))
+            if i >= 2:
+                layer2(i - 2)
+        layer2(SLICES - 2)
+        layer2(SLICES - 1)
+
+        terms = []
+        for d in range(D):
+            term = keep.tile([P, V], F32, name=f"term{d}")
+            terms.append(term)
+        part = keep.tile([P, V], F32, name="part")
+        total = keep.tile([P, V], F32, name="total")
+        halves = (slice(0, V // 2), slice(V // 2, V))
+
+        def fetch(d, cols):
+            nc.vector.tensor_tensor(
+                terms[d][:, cols],
+                y[:].indirect(places[d][:, cols.start // 16 : cols.stop // 16]),
+                gates[:, d, cols],
+                MULT,
+            )
+
+        fetch(0, slice(0, V))
+        fetch(1, slice(0, V))
+        fetch(2, halves[0])
+        nc.vector.tensor_add(part[:], terms[0][:], terms[1][:])
+        fetch(2, halves[1])
+        for cols in halves:
+            nc.vector.tensor_add(total[:, cols], part[:, cols], terms[2][:, cols])
+            nc.sync.dma_start(out[:, cols], total[:, cols])

@@ -28,9 +28,7 @@ def tile_picked_sub_mlp_gelu_sub_e_kernel(
     nc = tc.nc
     with ExitStack() as ctx:
         keep = ctx.enter_context(tc.tile_pool(name="keep", bufs=1))
-        ring = ctx.enter_context(tc.tile_pool(name="ring", bufs=3))
         banks = ctx.enter_context(tc.psum_pool(name="banks", bufs=1))
-        ybanks = ctx.enter_context(tc.psum_pool(name="ybanks", bufs=2))
 
         dummy = keep.tile([P, 1], F32, name="dummy")
         nc.vector.memset(dummy[:], 0.0)
@@ -70,13 +68,12 @@ def tile_picked_sub_mlp_gelu_sub_e_kernel(
             x_codes.append(keep.tile([P, S], U32, align_bytes=64, name=f"x_codes{s}"))
             x_scales.append(keep.tile([P, S], U8, align_bytes=64, name=f"x_scales{s}"))
 
-        def quantise_x(s, grouped):
-            for a, b in ((0, 512), (512, 768)):
-                nc.vector.quantize_mx(
-                    out=x_codes[s][:, a:b].bitcast(FP8X4),
-                    scales=x_scales[s][:, a:b],
-                    in_=grouped[:, a:b, :].rearrange("p n t -> p (n t)"),
-                )
+        def quantise_x(s, grouped, a, b):
+            nc.vector.quantize_mx(
+                out=x_codes[s][:, a:b].bitcast(FP8X4),
+                scales=x_scales[s][:, a:b],
+                in_=grouped[:, a:b, :].rearrange("p n t -> p (n t)"),
+            )
 
         xg0 = keep.tile([P, S, PACK], BF16, align_bytes=64, name="xg0")
         xg1 = keep.tile([P, S, PACK], BF16, align_bytes=64, name="xg1")
@@ -91,10 +88,10 @@ def tile_picked_sub_mlp_gelu_sub_e_kernel(
         for t in range(2):
             nc.vector.tensor_copy(picked1[:, t, :], planes[4 + t][:].indirect(offsets[:]))
         nc.scalar.copy(xg1[:, :, 0:2], picked1[:].rearrange("p t n -> p n t"))
-        quantise_x(0, xg0)
-        for t in range(2, PACK):
-            nc.vector.tensor_copy(xg1[:, :, t], planes[4 + t][:].indirect(offsets[:]))
-        quantise_x(1, xg1)
+        quantise_x(0, xg0, 0, 512)
+        quantise_x(0, xg0, 512, 768)
+        nc.vector.tensor_copy(xg1[:, :, 2], planes[6][:].indirect(offsets[:]))
+        nc.vector.tensor_copy(xg1[:, 0:512, 3], planes[7][:].indirect(offsets[:, 0:32]))
 
         w1_codes = []
         w1_scales = []
@@ -105,9 +102,10 @@ def tile_picked_sub_mlp_gelu_sub_e_kernel(
             w1_grouped.append(keep.tile([P, PACK, P, PACK], BF16, align_bytes=64, name=f"w1_grouped{s}"))
 
         def group_w1(copy, s, u, a, b):
+            raw = w1_raw[2 * s + u][:].rearrange("p j (m t) -> p m t j", t=PACK)
             copy(
-                w1_grouped[s][:, :, a:b, 2 * u : 2 * u + 2].rearrange("p t m j -> p m t j"),
-                w1_raw[2 * s + u][:, :, PACK * a : PACK * b].rearrange("p j (m t) -> p m t j", t=PACK),
+                w1_grouped[s][:, a:b, :, 2 * u : 2 * u + 2].rearrange("p t m j -> p m t j"),
+                raw[:, :, a:b, :],
             )
 
         def quantise_w1(s):
@@ -118,28 +116,32 @@ def tile_picked_sub_mlp_gelu_sub_e_kernel(
                     in_=w1_grouped[s][:, a:b].rearrange("p t m j -> p (t m j)"),
                 )
 
-        group_w1(nc.scalar.copy, 0, 0, 0, P)
-        group_w1(nc.scalar.copy, 0, 1, 0, 64)
-        group_w1(nc.vector.tensor_copy, 0, 1, 64, P)
+        group_w1(nc.scalar.copy, 0, 0, 0, 4)
+        group_w1(nc.scalar.copy, 0, 1, 2, 4)
+        group_w1(nc.vector.tensor_copy, 0, 1, 0, 2)
+        quantise_x(1, xg1, 0, 512)
         quantise_w1(0)
-        group_w1(nc.scalar.copy, 1, 0, 0, P)
-        group_w1(nc.scalar.copy, 1, 1, 0, 40)
-        group_w1(nc.vector.tensor_copy, 1, 1, 40, P)
+        group_w1(nc.vector.tensor_copy, 1, 0, 0, 2)
+        group_w1(nc.scalar.copy, 1, 0, 2, 4)
+        group_w1(nc.scalar.copy, 1, 1, 2, 4)
+        group_w1(nc.vector.tensor_copy, 1, 1, 0, 2)
         quantise_w1(1)
+        nc.vector.tensor_copy(xg1[:, 512:768, 3], planes[7][:].indirect(offsets[:, 32:48]))
 
         w2_grouped = keep.tile([P, N, PACK], BF16, align_bytes=64, name="w2_grouped")
         w2_codes = keep.tile([P, N], U32, align_bytes=64, name="w2_codes")
         w2_scales = keep.tile([P, N], U8, align_bytes=64, name="w2_scales")
-        nc.vector.tensor_copy(w2_grouped[:], w2_raw[:].rearrange("p j n -> p n j"))
+        nc.scalar.copy(w2_grouped[:], w2_raw[:].rearrange("p j n -> p n j"))
         nc.vector.quantize_mx(
             out=w2_codes[:].bitcast(FP8X4),
             scales=w2_scales[:],
             in_=w2_grouped[:].rearrange("p n j -> p (n j)"),
         )
+        quantise_x(1, xg1, 512, 768)
 
         acc = []
         for i in range(SLICES):
-            acc.append(banks.tile([P, PACK, SLICE], F32, name=f"acc{i}"))
+            acc.append(banks.tile([P, PACK, SLICE], F32, name=f"acc{i}", tag=f"acc{i}"))
 
         def layer1(i, t, s):
             cols = slice(i * SLICE, (i + 1) * SLICE)
@@ -153,25 +155,8 @@ def tile_picked_sub_mlp_gelu_sub_e_kernel(
                 stop=(s == PASSES - 1),
             )
 
-        y = keep.tile([P, S], F32, name="y")
-        hidden = []
-
-        def layer2(i):
-            h_codes, h_scales = hidden[i]
-            y_bank = ybanks.tile([P, SLICE], F32, name="y_bank")
-            nc.tensor.matmul_mx(
-                out=y_bank[:],
-                lhsT=w2_codes[:].bitcast(FP8X4),
-                lhsT_scale=w2_scales[:],
-                rhs=h_codes[:].bitcast(FP8X4),
-                rhs_scale=h_scales[:],
-                start=True,
-                stop=True,
-            )
-            nc.vector.tensor_copy(y[:, i * SLICE : (i + 1) * SLICE], y_bank[:])
-
         for r in range(3):
-            warm = ybanks.tile([P, 512], F32, name="y_bank")
+            warm = banks.tile([P, 512], F32, name="warm", tag="y1")
             nc.tensor.matmul_mx(
                 out=warm[:],
                 lhsT=x_codes[0][:, 0:P].bitcast(FP8X4),
@@ -183,25 +168,42 @@ def tile_picked_sub_mlp_gelu_sub_e_kernel(
             )
         for i in range(SLICES):
             layer1(i, 0, 0)
+        hidden = []
         for i in range(SLICES):
             layer1(i, 0, 1)
             for t in range(1, PACK):
                 for s in range(PASSES):
                     layer1(i, t, s)
-            h = ring.tile([P, SLICE, PACK], BF16, align_bytes=64, name="h")
+            h = keep.tile([P, SLICE, PACK], BF16, align_bytes=64, name=f"h{i}")
             nc.scalar.activation(h[:], acc[i][:].rearrange("p t n -> p n t"), GELU)
-            h_codes = ring.tile([P, SLICE], U32, align_bytes=64, name="h_codes")
-            h_scales = ring.tile([P, SLICE], U8, align_bytes=64, name="h_scales")
+            h_codes = keep.tile([P, SLICE], U32, align_bytes=64, name=f"h_codes{i}")
+            h_scales = keep.tile([P, SLICE], U8, align_bytes=64, name=f"h_scales{i}")
             nc.vector.quantize_mx(
                 out=h_codes[:].bitcast(FP8X4),
                 scales=h_scales[:],
                 in_=h[:].rearrange("p n t -> p (n t)"),
             )
             hidden.append((h_codes, h_scales))
-            if i >= 2:
-                layer2(i - 2)
-        layer2(SLICES - 2)
-        layer2(SLICES - 1)
+
+        y = keep.tile([P, S], F32, name="y")
+        y_main = banks.tile([P, 4, SLICE], F32, name="y_main", tag="y0")
+        y_fifth = banks.tile([P, SLICE], F32, name="y_fifth", tag="y1")
+        y_last = banks.tile([P, SLICE], F32, name="y_last", tag="acc0")
+        y_parts = [y_main[:, i, :] for i in range(4)] + [y_fifth[:], y_last[:]]
+        for i in range(SLICES):
+            h_codes, h_scales = hidden[i]
+            nc.tensor.matmul_mx(
+                out=y_parts[i],
+                lhsT=w2_codes[:].bitcast(FP8X4),
+                lhsT_scale=w2_scales[:],
+                rhs=h_codes[:].bitcast(FP8X4),
+                rhs_scale=h_scales[:],
+                start=True,
+                stop=True,
+            )
+        nc.scalar.copy(y[:, 0 : 4 * SLICE], y_main[:].rearrange("p i n -> p (i n)"))
+        nc.vector.tensor_copy(y[:, 4 * SLICE : 5 * SLICE], y_fifth[:])
+        nc.vector.tensor_copy(y[:, 5 * SLICE : 6 * SLICE], y_last[:])
 
         terms = []
         for d in range(D):

@@ -128,15 +128,6 @@ def tile_picked_sub_mlp_gelu_sub_e_kernel(
         quantise_w1(1)
         nc.vector.tensor_copy(xg1[:, 512:768, 3], planes[7][:].indirect(offsets[:, 32:48]))
 
-        w2_grouped = keep.tile([P, N, PACK], BF16, align_bytes=64, name="w2_grouped")
-        w2_codes = keep.tile([P, N], U32, align_bytes=64, name="w2_codes")
-        w2_scales = keep.tile([P, N], U8, align_bytes=64, name="w2_scales")
-        nc.scalar.copy(w2_grouped[:], w2_raw[:].rearrange("p j n -> p n j"))
-        nc.vector.quantize_mx(
-            out=w2_codes[:].bitcast(FP8X4),
-            scales=w2_scales[:],
-            in_=w2_grouped[:].rearrange("p n j -> p (n j)"),
-        )
         quantise_x(1, xg1, 512, 768)
 
         acc = []
@@ -166,6 +157,9 @@ def tile_picked_sub_mlp_gelu_sub_e_kernel(
                 start=True,
                 stop=True,
             )
+        w2_grouped = keep.tile([P, N, PACK], BF16, align_bytes=64, name="w2_grouped")
+        w2_codes = keep.tile([P, N], U32, align_bytes=64, name="w2_codes")
+        w2_scales = keep.tile([P, N], U8, align_bytes=64, name="w2_scales")
         for i in range(SLICES):
             layer1(i, 0, 0)
         hidden = []
@@ -184,6 +178,14 @@ def tile_picked_sub_mlp_gelu_sub_e_kernel(
                 in_=h[:].rearrange("p n t -> p (n t)"),
             )
             hidden.append((h_codes, h_scales))
+            if i == 1:
+                nc.vector.tensor_copy(w2_grouped[:], w2_raw[:].rearrange("p j n -> p n j"))
+            if i == 2:
+                nc.vector.quantize_mx(
+                    out=w2_codes[:].bitcast(FP8X4),
+                    scales=w2_scales[:],
+                    in_=w2_grouped[:].rearrange("p n j -> p (n j)"),
+                )
 
         y = keep.tile([P, S], F32, name="y")
         y_main = banks.tile([P, 4, SLICE], F32, name="y_main", tag="y0")
@@ -203,7 +205,7 @@ def tile_picked_sub_mlp_gelu_sub_e_kernel(
             )
         nc.scalar.copy(y[:, 0 : 4 * SLICE], y_main[:].rearrange("p i n -> p (i n)"))
         nc.vector.tensor_copy(y[:, 4 * SLICE : 5 * SLICE], y_fifth[:])
-        nc.vector.tensor_copy(y[:, 5 * SLICE : 6 * SLICE], y_last[:])
+        nc.scalar.copy(y[:, 5 * SLICE : 6 * SLICE], y_last[:])
 
         terms = []
         for d in range(D):

@@ -116,9 +116,11 @@ def tile_picked_sub_mlp_gelu_sub_e_kernel(
                     in_=w1_grouped[s][:, a:b].rearrange("p t m j -> p (t m j)"),
                 )
 
-        group_w1(nc.scalar.copy, 0, 0, 0, 4)
-        group_w1(nc.scalar.copy, 0, 1, 2, 4)
-        group_w1(nc.vector.tensor_copy, 0, 1, 0, 2)
+        def gpsimd_copy(dst, src):
+            nc.gpsimd.tensor_scalar(dst, src, 1.0, 0.0, MULT, mybir.AluOpType.add)
+
+        group_w1(gpsimd_copy, 0, 0, 0, 4)
+        group_w1(nc.scalar.copy, 0, 1, 0, 4)
         quantise_x(1, xg1, 0, 512)
         quantise_w1(0)
         group_w1(nc.vector.tensor_copy, 1, 0, 0, 2)

from contextlib import ExitStack

import concourse.mybir as mybir

K, T, D, S, V, H, N = 1024, 2048, 3, 768, 384, 512, 128
FLOPS = 2 * K * H * S + 2 * H * N * S

F32 = mybir.dt.float32
BF16 = mybir.dt.bfloat16
U32 = mybir.dt.uint32
U16 = mybir.dt.uint16
U8 = mybir.dt.uint8
FP8X4 = mybir.dt.float8_e4m3fn_x4
MULT = mybir.AluOpType.mult
GELU = mybir.ActivationFunctionType.Gelu_apprx_tanh

P = 128
PACK = 4
K_PASS = P * PACK
PASSES = K // K_PASS
SLICE = 128
SLICES = S // SLICE


def tile_picked_sub_mlp_gelu_sub_e_kernel(
    tc, xT, w1, w2, gate, offs, pos1, pos2, pos3, out
):
    nc = tc.nc
    with ExitStack() as ctx:
        keep = ctx.enter_context(tc.tile_pool(name="keep", bufs=1))
        banks = ctx.enter_context(tc.psum_pool(name="banks", bufs=1))

        dummy = keep.tile([P, 1], F32, name="dummy")
        nc.vector.memset(dummy[:], 0.0)
        dummy_out = keep.tile([P, 1], F32, name="dummy_out")
        nc.scalar.activation(dummy_out[:], dummy[:], GELU)

        planes = []
        offsets = keep.tile([P, S // 16], U16, name="offsets")
        for s in range(PASSES):
            rows = xT[s * K_PASS : (s + 1) * K_PASS, :].rearrange("(p t) c -> p t c", t=PACK)
            for t in range(PACK):
                plane = keep.tile([P, T], F32, name=f"plane{s}{t}")
                nc.sync.dma_start(plane[:], rows[:, t, :])
                planes.append(plane)
                if s == 0 and t == 0:
                    nc.sync.dma_start(offsets[:], offs)
        w1_raw = []
        for s in range(PASSES):
            rows = w1[s * K_PASS : (s + 1) * K_PASS, :].rearrange("(p j) c -> p j c", j=PACK)
            for u in range(2):
                raw = keep.tile([P, 2, H], F32, name=f"w1raw{s}{u}")
                nc.sync.dma_start(raw[:], rows[:, 2 * u : 2 * u + 2, :])
                w1_raw.append(raw)
        w2_raw = keep.tile([P, PACK, N], F32, name="w2_raw")
        nc.sync.dma_start(w2_raw[:], w2.rearrange("(p j) n -> p j n", j=PACK))
        places = []
        for d, pos in enumerate((pos1, pos2, pos3)):
            place = keep.tile([P, V // 16], U16, name=f"place{d}")
            nc.sync.dma_start(place[:], pos)
            places.append(place)
        gates = keep.tile([P, D, V], F32, name="gates")
        nc.sync.dma_start(gates[:], gate.rearrange("d m v -> m d v"))

        x_codes = []
        x_scales = []
        for s in range(PASSES):
            x_codes.append(keep.tile([P, S], U32, align_bytes=64, name=f"x_codes{s}"))
            x_scales.append(keep.tile([P, S], U8, align_bytes=64, name=f"x_scales{s}"))

        def quantise_x(s, grouped, a, b):
            nc.vector.quantize_mx(
                out=x_codes[s][:, a:b].bitcast(FP8X4),
                scales=x_scales[s][:, a:b],
                in_=grouped[:, a:b, :].rearrange("p n t -> p (n t)"),
            )

        xg0 = keep.tile([P, S, PACK], BF16, align_bytes=64, name="xg0")
        xg1 = keep.tile([P, S, PACK], BF16, align_bytes=64, name="xg1")
        picked0 = keep.tile([P, PACK, S], F32, name="picked0")
        picked1 = keep.tile([P, 2, S], F32, name="picked1")
        for t in range(PACK):
            nc.vector.tensor_copy(picked0[:, t, :], planes[t][:].indirect(offsets[:]))
        nc.scalar.copy(
            xg0[:].rearrange("p (c i) t -> p c t i", i=4),
            picked0[:].rearrange("p t (c i) -> p c t i", i=4),
        )
        for t in range(2):
            nc.vector.tensor_copy(picked1[:, t, :], planes[4 + t][:].indirect(offsets[:]))
        nc.scalar.copy(xg1[:, :, 0:2], picked1[:].rearrange("p t n -> p n t"))
        quantise_x(0, xg0, 0, 512)
        quantise_x(0, xg0, 512, 768)
        nc.vector.tensor_copy(xg1[:, :, 2], planes[6][:].indirect(offsets[:]))
        nc.vector.tensor_copy(xg1[:, 0:512, 3], planes[7][:].indirect(offsets[:, 0:32]))

        w1_codes = []
        w1_scales = []
        w1_grouped = []
        for s in range(PASSES):
            w1_codes.append(keep.tile([P, H], U32, align_bytes=64, name=f"w1_codes{s}"))
            w1_scales.append(keep.tile([P, H], U8, align_bytes=64, name=f"w1_scales{s}"))
            w1_grouped.append(keep.tile([P, PACK, P, PACK], BF16, align_bytes=64, name=f"w1_grouped{s}"))

        def group_w1(copy, s, u, a, b):
            raw = w1_raw[2 * s + u][:].rearrange("p j (m t) -> p m t j", t=PACK)
            copy(
                w1_grouped[s][:, a:b, :, 2 * u : 2 * u + 2].rearrange("p t m j -> p m t j"),
                raw[:, :, a:b, :],
            )

        def quantise_w1(s):
            for a, b in ((0, 2), (2, 4)):
                nc.vector.quantize_mx(
                    out=w1_codes[s][:, P * a : P * b].bitcast(FP8X4),
                    scales=w1_scales[s][:, P * a : P * b],
                    in_=w1_grouped[s][:, a:b].rearrange("p t m j -> p (t m j)"),
                )

        def gpsimd_copy(dst, src):
            nc.gpsimd.tensor_scalar(dst, src, 1.0, 0.0, MULT, mybir.AluOpType.add)

        group_w1(gpsimd_copy, 0, 0, 0, 4)
        group_w1(nc.scalar.copy, 0, 1, 0, 4)
        quantise_x(1, xg1, 0, 512)
        quantise_w1(0)
        group_w1(nc.vector.tensor_copy, 1, 0, 0, 2)
        group_w1(nc.scalar.copy, 1, 0, 2, 4)
        group_w1(nc.scalar.copy, 1, 1, 2, 4)
        group_w1(nc.vector.tensor_copy, 1, 1, 0, 2)
        quantise_w1(1)
        nc.vector.tensor_copy(xg1[:, 512:768, 3], planes[7][:].indirect(offsets[:, 32:48]))

        quantise_x(1, xg1, 512, 768)

        acc = []
        for i in range(SLICES):
            acc.append(banks.tile([P, PACK, SLICE], F32, name=f"acc{i}", tag=f"acc{i}"))

        def layer1(i, t, s):
            cols = slice(i * SLICE, (i + 1) * SLICE)
            nc.tensor.matmul_mx(
                out=acc[i][:, t, :],
                lhsT=w1_codes[s][:, t * P : (t + 1) * P].bitcast(FP8X4),
                lhsT_scale=w1_scales[s][:, t * P : (t + 1) * P],
                rhs=x_codes[s][:, cols].bitcast(FP8X4),
                rhs_scale=x_scales[s][:, cols],
                start=(s == 0),
                stop=(s == PASSES - 1),
            )

        for r in range(3):
            warm = banks.tile([P, 512], F32, name="warm", tag="y1")
            nc.tensor.matmul_mx(
                out=warm[:],
                lhsT=x_codes[0][:, 0:P].bitcast(FP8X4),
                lhsT_scale=x_scales[0][:, 0:P],
                rhs=x_codes[1][:, 0:512].bitcast(FP8X4),
                rhs_scale=x_scales[1][:, 0:512],
                start=True,
                stop=True,
            )
        w2_grouped = keep.tile([P, N, PACK], BF16, align_bytes=64, name="w2_grouped")
        w2_codes = keep.tile([P, N], U32, align_bytes=64, name="w2_codes")
        w2_scales = keep.tile([P, N], U8, align_bytes=64, name="w2_scales")
        for i in range(SLICES):
            layer1(i, 0, 0)
        hidden = []
        for i in range(SLICES):
            layer1(i, 0, 1)
            for t in range(1, PACK):
                for s in range(PASSES):
                    layer1(i, t, s)
            h = keep.tile([P, SLICE, PACK], BF16, align_bytes=64, name=f"h{i}")
            nc.scalar.activation(h[:], acc[i][:].rearrange("p t n -> p n t"), GELU)
            h_codes = keep.tile([P, SLICE], U32, align_bytes=64, name=f"h_codes{i}")
            h_scales = keep.tile([P, SLICE], U8, align_bytes=64, name=f"h_scales{i}")
            nc.vector.quantize_mx(
                out=h_codes[:].bitcast(FP8X4),
                scales=h_scales[:],
                in_=h[:].rearrange("p n t -> p (n t)"),
            )
            hidden.append((h_codes, h_scales))
            if i == 1:
                nc.vector.tensor_copy(w2_grouped[:], w2_raw[:].rearrange("p j n -> p n j"))
            if i == 2:
                nc.vector.quantize_mx(
                    out=w2_codes[:].bitcast(FP8X4),
                    scales=w2_scales[:],
                    in_=w2_grouped[:].rearrange("p n j -> p (n j)"),
                )

        y = keep.tile([P, S], F32, name="y")
        y_main = banks.tile([P, 4, SLICE], F32, name="y_main", tag="y0")
        y_fifth = banks.tile([P, SLICE], F32, name="y_fifth", tag="y1")
        y_last = banks.tile([P, SLICE], F32, name="y_last", tag="acc0")
        y_parts = [y_main[:, i, :] for i in range(4)] + [y_fifth[:], y_last[:]]
        for i in range(SLICES):
            h_codes, h_scales = hidden[i]
            nc.tensor.matmul_mx(
                out=y_parts[i],
                lhsT=w2_codes[:].bitcast(FP8X4),
                lhsT_scale=w2_scales[:],
                rhs=h_codes[:].bitcast(FP8X4),
                rhs_scale=h_scales[:],
                start=True,
                stop=True,
            )
        nc.scalar.copy(y[:, 0 : 4 * SLICE], y_main[:].rearrange("p i n -> p (i n)"))
        nc.vector.tensor_copy(y[:, 4 * SLICE : 5 * SLICE], y_fifth[:])
        nc.scalar.copy(y[:, 5 * SLICE : 6 * SLICE], y_last[:])

        terms = []
        for d in range(D):
            term = keep.tile([P, V], F32, name=f"term{d}")
            terms.append(term)
        part = keep.tile([P, V], F32, name="part")
        total = keep.tile([P, V], F32, name="total")
        halves = (slice(0, V // 2), slice(V // 2, V))

        def fetch(d, cols):
            nc.vector.tensor_tensor(
                terms[d][:, cols],
                y[:].indirect(places[d][:, cols.start // 16 : cols.stop // 16]),
                gates[:, d, cols],
                MULT,
            )

        fetch(0, slice(0, V))
        fetch(1, slice(0, V))
        fetch(2, halves[0])
        nc.vector.tensor_add(part[:], terms[0][:], terms[1][:])
        fetch(2, halves[1])
        for cols in halves:
            nc.vector.tensor_add(total[:, cols], part[:, cols], terms[2][:, cols])
            nc.sync.dma_start(out[:, cols], total[:, cols])
